import numpy as np
import ml_dtypes


def mxq(x, axis, fmt="e4m3"):
    dtype, down = {"e4m3": (ml_dtypes.float8_e4m3fn, 7), "e5m2": (ml_dtypes.float8_e5m2, 14)}[fmt]
    v = np.moveaxis(np.asarray(x, np.float32).astype(ml_dtypes.bfloat16).astype(np.float64), axis, -1)
    blocks = v.reshape(v.shape[:-1] + (-1, 32))
    amax = np.abs(blocks).max(-1, keepdims=True)
    byte = np.maximum(np.where(amax > 0, np.frexp(amax)[1] - 1 + 127, 0) - down, 1)
    scale = np.exp2(byte - 127.0)
    codes = (blocks / scale).astype(np.float32).astype(dtype).astype(np.float64)
    return np.moveaxis((codes * scale).reshape(v.shape), -1, axis)


WIDE = False


def mx_kscale(k):
    if not WIDE:
        return np.ones(k)
    levels = np.array([10, -10, 5, -5, 0])
    if k % 512:
        return np.exp2(np.random.permutation(np.resize(levels, k // 32))).repeat(32)
    a = np.empty((k // 512, 16))
    for p in range(k // 512):
        a[p, :8] = np.random.permutation(np.resize(levels, 8))
        for g in range(8):
            far = levels[np.abs(levels - a[p, g]) >= 10]
            a[p, g + 8] = far[np.random.randint(len(far))]
    return np.exp2(a.ravel()).repeat(32)


BF16 = ml_dtypes.bfloat16


def bf(x):
    return np.asarray(x, np.float32).astype(BF16)


def f64(x):
    return np.asarray(x).astype(np.float64)

def planes(Y):
    n, m = Y.shape
    b = f64(bf(Y)).reshape(n // 32, 32, m)
    amax = np.abs(b).max(1)
    byte = np.clip(np.where(amax > 0, np.frexp(amax)[1] - 1 + 127 - 7, 1), 1, 254)
    codes = (b * np.exp2(127.0 - byte)[:, None, :]).reshape(n, m).astype(np.float32).astype(ml_dtypes.float8_e4m3fn).view(np.uint8)
    words = codes.reshape(n // 512, 128, 4, m).transpose(0, 1, 3, 2)
    return np.ascontiguousarray(words), np.ascontiguousarray(byte.astype(np.uint8).reshape(n // 512, 16, m))


H, L, D, N = 16, 128, 1024, 2048
CAP = 3.0


def setup_inputs():
    s = mx_kscale(D)
    length = np.exp(0.4 * np.random.randn(N, 1))
    keys = length * np.random.randn(N, D)
    prefer = np.random.randn(H, 1, D)
    queries = prefer + 0.7 * np.random.randn(H, L, D)
    cap = CAP * (1.0 + 0.1 * np.random.randn(H))
    slope = (1.0 + 0.1 * np.random.randn(H)) / (CAP * np.sqrt(D))
    return {
        "queries": bf(queries / s),
        "keys": bf(keys * s),
        "slope": bf(slope),
        "cap": bf(cap),
    }


def reference(queries, keys, slope, cap):
    qq = mxq(f64(queries).reshape(H * L, D), 1, "e4m3")
    kq = mxq(f64(keys), 1, "e4m3")
    scores = (kq @ qq.T).reshape(N, H, L)
    a = f64(slope).reshape(1, H, 1)
    c = f64(cap).reshape(1, H, 1)
    y = np.exp(c * np.tanh(a * scores))
    Y = y.reshape(N, H * L)
    words, scales = planes(Y)
    return y, words, scales

@@ -1,0 +1,219 @@
+from contextlib import ExitStack
+
+import concourse.mybir as mybir
+from concourse.masks import make_identity
+
+H, L, D, N = 16, 128, 1024, 2048
+FLOPS = 2 * N * H * L * D
+
+F32 = mybir.dt.float32
+BF16 = mybir.dt.bfloat16
+I32 = mybir.dt.int32
+U32 = mybir.dt.uint32
+U8 = mybir.dt.uint8
+FP8X4 = mybir.dt.float8_e4m3fn_x4
+ACT = mybir.ActivationFunctionType
+
+P = 128
+PACK = 4
+PASSES = D // (P * PACK)
+GROUPS = N // (P * PACK)
+HEADS_PER_CHUNK = 4
+CHUNK = HEADS_PER_CHUNK * L
+
+CHUNKS = [(0, 0), (1, 0), (0, 1), (1, 1), (2, 0), (2, 1), (0, 2), (1, 2), (2, 2),
+          (3, 0), (3, 1), (3, 2), (0, 3), (1, 3), (2, 3), (3, 3)]
+HEAD_TILES = 12
+SCALAR_COPIES = 12
+OUT_LAG = 5
+
+
+def schedule():
+    keys = lambda g: [("k", g, t) for t in range(PACK)]
+    heads = lambda a, b: [("q", h) for h in range(a, b)]
+    tiles = (heads(0, 1) + keys(0) + heads(1, 4) + keys(1) + heads(4, 8) + keys(2)
+             + heads(8, 12) + keys(3) + heads(12, 16))
+    units = [(g, HEADS_PER_CHUNK * c + j) for g, c in CHUNKS for j in range(HEADS_PER_CHUNK)]
+    ev = []
+    for i in range(HEAD_TILES):
+        ev.append(("transpose", tiles[i]))
+        ev.append(("copy", tiles[i], "scalar" if i < SCALAR_COPIES else "vector"))
+        ev.append(("quant", tiles[i]))
+    done = HEAD_TILES
+    pending = []
+    n_cast = n_planes = 0
+    for u in range(len(units) + 2):
+        fresh = []
+        if u < len(units):
+            if u % 3 == 2:
+                fresh = tiles[done : done + 2]
+                done += len(fresh)
+            for x in fresh:
+                ev.append(("transpose", x))
+            ev.append(("matmul", u))
+            ev.append(("tanh", u))
+        late = done == len(tiles) and not fresh and not pending
+        if late:
+            while n_planes < n_cast:
+                ev.append(("planes", n_planes))
+                n_planes += 1
+        if 1 <= u <= len(units):
+            ev.append(("exp", u - 1))
+        for x in fresh:
+            ev.append(("copy", x, "vector"))
+        planes_due = n_cast
+        while n_cast < min(len(units), u if late else u - OUT_LAG + 1):
+            ev.append(("cast", n_cast))
+            n_cast += 1
+        for x in pending:
+            ev.append(("quant", x))
+        pending = fresh
+        while n_planes < planes_due:
+            ev.append(("planes", n_planes))
+            n_planes += 1
+    return tiles, units, ev
+
+
+def tile_softcap_multiquery_exp_scores_g2_kernel(tc, queries, keys, slope, cap, out_0, out_1, out_2):
+    nc = tc.nc
+    tiles, units, events = schedule()
+    last_chunk = len(CHUNKS) - 1
+
+    y_hbm = out_0.rearrange("(g p t) h l -> g p t (h l)", p=P, t=PACK)
+    words_hbm = out_1.rearrange("g p m t -> g p (m t)").bitcast(I32)
+    scales_hbm = out_2.bitcast(I32)
+    keys_hbm = keys.rearrange("(g p t) d -> g p t d", p=P, t=PACK)
+    queries_hbm = queries.rearrange("h l d -> l h d")
+
+    with ExitStack() as ctx:
+        keep = ctx.enter_context(tc.tile_pool(name="keep", bufs=1))
+        work = ctx.enter_context(tc.tile_pool(name="work", bufs=3))
+        psum = ctx.enter_context(tc.psum_pool(name="psum", bufs=4))
+        ctx.enter_context(tc.manual_schedule())
+
+        ident = keep.tile([P, P], F32, name="ident")
+        make_identity(nc, ident[:])
+        slope_raw = keep.tile([P, H], BF16, name="slope_raw")
+        cap_raw = keep.tile([P, H], BF16, name="cap_raw")
+        slope_f = keep.tile([P, H], F32, name="slope_f")
+        cap_f = keep.tile([P, H], F32, name="cap_f")
+        warm = keep.tile([P, 1], F32, name="warm")
+        nc.scalar.dma_start(out=slope_raw[:], in_=slope.partition_broadcast(P))
+        nc.scalar.dma_start(out=cap_raw[:], in_=cap.partition_broadcast(P))
+        nc.scalar.activation(out=warm[:], in_=ident[:, 0:1], func=ACT.Exp)
+
+        k_raw = keep.tile([P, GROUPS, PACK, D], BF16, name="k_raw")
+        q_raw = keep.tile([P, H, D], BF16, name="q_raw")
+        k_codes = keep.tile([P, GROUPS, PACK, PASSES * P], U32, name="k_codes", align_bytes=64)
+        k_scales = keep.tile([P, GROUPS, PACK, PASSES * P], U8, name="k_scales", align_bytes=64)
+        q_codes = keep.tile([P, H, PASSES * P], U32, name="q_codes", align_bytes=64)
+        q_scales = keep.tile([P, H, PASSES * P], U8, name="q_scales", align_bytes=64)
+        y_scales = keep.tile([P, GROUPS, H * L], U8, name="y_scales", align_bytes=64)
+
+        def pick(x, k_tile, q_tile):
+            return k_tile[:, x[1], x[2], :] if x[0] == "k" else q_tile[:, x[1], :]
+
+        for i, x in enumerate(tiles):
+            if i < 16:
+                src = keys_hbm[x[1], :, x[2], :] if x[0] == "k" else queries_hbm[:, x[1], :]
+                nc.sync.dma_start(out=pick(x, k_raw, q_raw), in_=src)
+            elif i % 4 == 0:
+                if x[0] == "k":
+                    nc.sync.dma_start(out=k_raw[:, x[1], :, :], in_=keys_hbm[x[1]])
+                else:
+                    nc.sync.dma_start(out=q_raw[:, x[1] : x[1] + 4, :], in_=queries_hbm[:, x[1] : x[1] + 4, :])
+
+        nc.vector.tensor_copy(out=slope_f[:], in_=slope_raw[:])
+        nc.vector.tensor_copy(out=cap_f[:], in_=cap_raw[:])
+
+        turned, grouped, scores, capped, y, y_bf, y_codes = {}, {}, {}, {}, {}, {}, {}
+
+        def store_scales(m0, m1):
+            for quad in range(4):
+                eng = nc.sync if quad % 2 == 0 or m1 < H * L else nc.scalar
+                eng.dma_start(
+                    out=scales_hbm[:, 4 * quad : 4 * quad + 4, m0 // 4 : m1 // 4].rearrange("g r w -> r g w"),
+                    in_=y_scales[32 * quad : 32 * quad + 4, :, m0:m1].bitcast(I32),
+                )
+
+        for ev in events:
+            kind = ev[0]
+            if kind == "transpose":
+                x = ev[1]
+                words = pick(x, k_raw, q_raw).bitcast(F32)
+                turned[x] = psum.tile([P, PASSES, 2, P], F32, name="turned", tag="turned")
+                for c in range(PASSES):
+                    for u in range(2):
+                        nc.tensor.transpose(turned[x][:, c, u, :], words[:, 256 * c + u : 256 * (c + 1) : 2], ident[:])
+            elif kind == "copy":
+                x = ev[1]
+                grouped[x] = work.tile([P, D], BF16, name="grouped", tag="grouped", bufs=4, align_bytes=64)
+                dst = grouped[x][:].bitcast(F32).rearrange("p (c r u) -> p c r u", c=PASSES, u=2)
+                src = turned[x][:].rearrange("p c u r -> p c r u")
+                if ev[2] == "scalar":
+                    nc.scalar.copy(out=dst, in_=src)
+                else:
+                    nc.vector.tensor_copy(out=dst, in_=src)
+            elif kind == "quant":
+                x = ev[1]
+                nc.vector.quantize_mx(out=pick(x, k_codes, q_codes).bitcast(FP8X4), scales=pick(x, k_scales, q_scales), in_=grouped[x][:])
+            elif kind == "matmul":
+                g, h = units[ev[1]]
+                scores[ev[1]] = psum.tile([P, PACK, L], F32, name="scores", tag="scores")
+                for t in range(PACK):
+                    for c in range(PASSES):
+                        cols = slice(c * P, (c + 1) * P)
+                        nc.tensor.matmul_mx(
+                            out=scores[ev[1]][:, t, :],
+                            lhsT=k_codes[:, g, t, cols].bitcast(FP8X4),
+                            lhsT_scale=k_scales[:, g, t, cols],
+                            rhs=q_codes[:, h, cols].bitcast(FP8X4),
+                            rhs_scale=q_scales[:, h, cols],
+                            start=(c == 0),
+                            stop=(c == PASSES - 1),
+                        )
+            elif kind == "tanh":
+                g, h = units[ev[1]]
+                capped[ev[1]] = work.tile([P, PACK, L], F32, name="capped", tag="capped", bufs=3)
+                nc.scalar.activation(out=capped[ev[1]][:], in_=scores[ev[1]][:], func=ACT.Tanh, scale=slope_f[:, h : h + 1])
+            elif kind == "exp":
+                g, h = units[ev[1]]
+                chunk, j = divmod(ev[1], HEADS_PER_CHUNK)
+                if j == 0:
+                    y[chunk] = work.tile([P, PACK, CHUNK], F32, name="y", tag="y", bufs=6)
+                nc.scalar.activation(out=y[chunk][:, :, j * L : (j + 1) * L], in_=capped[ev[1]][:], func=ACT.Exp, scale=cap_f[:, h : h + 1])
+                m0 = (h - j) * L
+                if chunk == last_chunk:
+                    nc.sync.dma_start(out=y_hbm[g, :, :, h * L : (h + 1) * L], in_=y[chunk][:, :, j * L : (j + 1) * L])
+                elif j == HEADS_PER_CHUNK - 1:
+                    nc.sync.dma_start(out=y_hbm[g, :, :, m0 : m0 + CHUNK], in_=y[chunk][:])
+            elif kind == "cast":
+                chunk, j = divmod(ev[1], HEADS_PER_CHUNK)
+                if j == 0:
+                    y_bf[chunk] = work.tile([P, CHUNK, PACK], BF16, name="y_bf", tag="y_bf", bufs=3, align_bytes=64)
+                nc.vector.tensor_copy(
+                    out=y_bf[chunk][:, j * L : (j + 1) * L, :],
+                    in_=y[chunk][:, :, j * L : (j + 1) * L].rearrange("p t m -> p m t"),
+                )
+            else:
+                g, h = units[ev[1]]
+                chunk, j = divmod(ev[1], HEADS_PER_CHUNK)
+                m0 = (h - j) * L
+                if chunk == last_chunk:
+                    lo, hi = j * L, (j + 1) * L
+                elif j == HEADS_PER_CHUNK - 1:
+                    lo, hi = 0, CHUNK
+                else:
+                    continue
+                if lo == 0:
+                    y_codes[chunk] = work.tile([P, CHUNK], U32, name="y_codes", tag="y_codes", bufs=3, align_bytes=64)
+                nc.vector.quantize_mx(
+                    out=y_codes[chunk][:, lo:hi].bitcast(FP8X4),
+                    scales=y_scales[:, g, m0 + lo : m0 + hi],
+                    in_=y_bf[chunk][:, lo:hi, :].rearrange("p m t -> p (m t)"),
+                )
+                nc.sync.dma_start(out=words_hbm[g, :, m0 + lo : m0 + hi], in_=y_codes[chunk][:, lo:hi].bitcast(I32))
+                if chunk == last_chunk - GROUPS:
+                    store_scales(0, m0 + CHUNK)
+                elif ev[1] == len(units) - 1:
+                    store_scales(m0, m0 + CHUNK)

@@ -12,72 +12,122 @@ I32 = mybir.dt.int32
 U32 = mybir.dt.uint32
 U8 = mybir.dt.uint8
 FP8X4 = mybir.dt.float8_e4m3fn_x4
-ACT = mybir.ActivationFunctionType
+FUNC = mybir.ActivationFunctionType
 
 P = 128
 PACK = 4
 PASSES = D // (P * PACK)
 GROUPS = N // (P * PACK)
-HEADS_PER_CHUNK = 4
-CHUNK = HEADS_PER_CHUNK * L
+CHUNK_HEADS = 4
+CHUNK = CHUNK_HEADS * L
+COLUMNS = H // CHUNK_HEADS
+BANKS, BANK_WIDTH = 8, 512
+QUADRANTS, SCALE_ROWS = 4, 4
 
-CHUNKS = [(0, 0), (1, 0), (0, 1), (1, 1), (2, 0), (2, 1), (0, 2), (1, 2), (2, 2),
-          (3, 0), (3, 1), (3, 2), (0, 3), (1, 3), (2, 3), (3, 3)]
-HEAD_TILES = 12
-SCALAR_COPIES = 12
-OUT_LAG = 5
+FIRST_TILES = 6
+SINGLE_LOADS = 16
+TILES_AFTER_FILL = {0: 4, 3: 3, 8: 3, 12: 4, 21: 2, 23: 2, 30: 2, 32: 2, 41: 2, 44: 2}
+SCALAR_TILES = (1, 2, 3, 6, 7, 12)
+SCORE_BANKS = 4
+LATE = 48
+RESULT_LAG = 7
+WARM_PASSES = 10
+WIDEN_AT, SPREAD_AT = 0, 3
 
 
-def schedule():
-    keys = lambda g: [("k", g, t) for t in range(PACK)]
-    heads = lambda a, b: [("q", h) for h in range(a, b)]
-    tiles = (heads(0, 1) + keys(0) + heads(1, 4) + keys(1) + heads(4, 8) + keys(2)
-             + heads(8, 12) + keys(3) + heads(12, 16))
-    units = [(g, HEADS_PER_CHUNK * c + j) for g, c in CHUNKS for j in range(HEADS_PER_CHUNK)]
-    ev = []
-    for i in range(HEAD_TILES):
-        ev.append(("transpose", tiles[i]))
-        ev.append(("copy", tiles[i], "scalar" if i < SCALAR_COPIES else "vector"))
-        ev.append(("quant", tiles[i]))
-    done = HEAD_TILES
-    pending = []
-    n_cast = n_planes = 0
-    for u in range(len(units) + 2):
-        fresh = []
-        if u < len(units):
-            if u % 3 == 2:
-                fresh = tiles[done : done + 2]
-                done += len(fresh)
-            for x in fresh:
-                ev.append(("transpose", x))
-            ev.append(("matmul", u))
-            ev.append(("tanh", u))
-        late = done == len(tiles) and not fresh and not pending
+def tile_order():
+    key_tiles = lambda g: [("k", g, t) for t in range(PACK)]
+    head_tiles = lambda c: [("q", h) for h in range(CHUNK_HEADS * c, CHUNK_HEADS * (c + 1))]
+    k0, q0 = key_tiles(0), head_tiles(0)
+    tiles = [k0[0], q0[0], k0[1], q0[1], k0[2], k0[3], q0[2], q0[3]] + key_tiles(1)
+    return tiles + head_tiles(1) + key_tiles(2) + head_tiles(2) + key_tiles(3) + head_tiles(3)
+
+
+def fill_order():
+    every_t = tuple(range(PACK))
+    halves = (every_t[:2], every_t[2:])
+    chunk_heads = lambda c: range(CHUNK_HEADS * c, CHUNK_HEADS * (c + 1))
+    chunk = lambda g, c: [(g, (h,), every_t) for h in chunk_heads(c)]
+    twin_chunks = lambda g, c: [(g + i, (h,), every_t) for h in chunk_heads(c) for i in range(2)]
+    fills = [(0, (0, 1), ts) for ts in halves] + chunk(0, 0)[2:]
+    fills += [(1, hs, ts) for ts in halves for hs in ((0, 1), (2, 3))]
+    fills += twin_chunks(0, 1) + chunk(2, 0) + chunk(2, 1) + twin_chunks(0, 2) + chunk(2, 2)
+    fills += chunk(3, 0) + chunk(3, 1) + chunk(3, 2)
+    for g in range(GROUPS):
+        fills += chunk(g, COLUMNS - 1)
+    return fills
+
+
+def first_twin(fills, f):
+    return f % 2 == 0 and fills[f][1:] == fills[f + 1][1:]
+
+
+def program(tiles, fills):
+    steps = []
+    emptier = lambda i: "scalar" if i in SCALAR_TILES else "vector"
+
+    for i in range(FIRST_TILES):
+        bank = BANKS - 1 - i
+        steps.append(("transpose", tiles[i], bank))
+        if i == SPREAD_AT:
+            steps.append(("spread",))
+        steps.append(("interleave", tiles[i], bank, emptier(i)))
+        if i == WIDEN_AT:
+            steps.append(("widen",))
+        steps.append(("quantise", tiles[i]))
+        if i == SPREAD_AT:
+            steps.append(("factors",))
+
+    n_tiles = FIRST_TILES
+    results = []
+    n_rounded = n_planes = 0
+    bank = -1
+    for f in range(len(fills) + 1):
+        late = f >= LATE
+        fresh = range(n_tiles, n_tiles + TILES_AFTER_FILL.get(f, 0))
+        n_tiles += len(fresh)
+        turn_bank = lambda i: BANKS - 1 - i % (BANKS - SCORE_BANKS)
+        if f < len(fills):
+            bank = (bank + 1) % (BANKS if late else SCORE_BANKS)
+            steps.append(("matmul", f, bank))
+            steps += [("transpose", tiles[i], turn_bank(i)) for i in fresh]
+            steps.append(("tanh", f, bank, 0))
+
+        planes_due = n_rounded
         if late:
-            while n_planes < n_cast:
-                ev.append(("planes", n_planes))
-                n_planes += 1
-        if 1 <= u <= len(units):
-            ev.append(("exp", u - 1))
-        for x in fresh:
-            ev.append(("copy", x, "vector"))
-        planes_due = n_cast
-        while n_cast < min(len(units), u if late else u - OUT_LAG + 1):
-            ev.append(("cast", n_cast))
-            n_cast += 1
-        for x in pending:
-            ev.append(("quant", x))
-        pending = fresh
-        while n_planes < planes_due:
-            ev.append(("planes", n_planes))
-            n_planes += 1
-    return tiles, units, ev
+            steps += [("planes", unit) for after, unit in results[n_planes:planes_due]]
+            n_planes = planes_due
+
+        if f >= 1 and not first_twin(fills, f - 1):
+            twins = f >= 2 and first_twin(fills, f - 2)
+            steps.append(("exp", f - 1, twins))
+            for g, hs, ts in fills[f - 2 if twins else f - 1 : f]:
+                if PACK - 1 in ts:
+                    results += [(f, (g, h)) for h in hs]
+        if f == len(fills) - 1:
+            steps.append(("tanh", f, bank, 1))
+
+        for k in range(len(fresh) + 1):
+            if k < len(fresh):
+                steps.append(("interleave", tiles[fresh[k]], turn_bank(fresh[k]), emptier(fresh[k])))
+            if k >= 1:
+                steps.append(("quantise", tiles[fresh[k - 1]]))
+
+        while n_rounded < len(results) and results[n_rounded][0] <= f - (0 if late else RESULT_LAG):
+            steps.append(("round", results[n_rounded][1]))
+            n_rounded += 1
+        steps += [("planes", unit) for after, unit in results[n_planes:planes_due]]
+        n_planes = planes_due
+    steps += [("planes", unit) for after, unit in results[n_planes:]]
+    return steps
 
 
 def tile_softcap_multiquery_exp_scores_g2_kernel(tc, queries, keys, slope, cap, out_0, out_1, out_2):
     nc = tc.nc
-    tiles, units, events = schedule()
-    last_chunk = len(CHUNKS) - 1
+    tiles, fills = tile_order(), fill_order()
+    last_fill = len(fills) - 1
+    last_chunk = (GROUPS - 1, COLUMNS - 1)
+    chunk_of = lambda g, h: (g, h // CHUNK_HEADS)
 
     y_hbm = out_0.rearrange("(g p t) h l -> g p t (h l)", p=P, t=PACK)
     words_hbm = out_1.rearrange("g p m t -> g p (m t)").bitcast(I32)
@@ -85,22 +135,52 @@ def tile_softcap_multiquery_exp_scores_g2_kernel(tc, queries, keys, slope, cap, 
     keys_hbm = keys.rearrange("(g p t) d -> g p t d", p=P, t=PACK)
     queries_hbm = queries.rearrange("h l d -> l h d")
 
+    home = {}
+    for f in range(0, len(fills), 2):
+        if first_twin(fills, f):
+            g, hs, ts = fills[f]
+            for place in range(2):
+                home[chunk_of(g + place, hs[0])] = (chunk_of(g, hs[0]), place, 2)
+    for g, hs, ts in fills:
+        home.setdefault(chunk_of(g, hs[0]), (chunk_of(g, hs[0]), 0, 1))
+
     with ExitStack() as ctx:
         keep = ctx.enter_context(tc.tile_pool(name="keep", bufs=1))
         work = ctx.enter_context(tc.tile_pool(name="work", bufs=3))
-        psum = ctx.enter_context(tc.psum_pool(name="psum", bufs=4))
+        psum = ctx.enter_context(tc.psum_pool(name="psum", bufs=1))
         ctx.enter_context(tc.manual_schedule())
 
+        banks = psum.tile([P, BANKS, BANK_WIDTH], F32, name="banks")
         ident = keep.tile([P, P], F32, name="ident")
         make_identity(nc, ident[:])
-        slope_raw = keep.tile([P, H], BF16, name="slope_raw")
-        cap_raw = keep.tile([P, H], BF16, name="cap_raw")
-        slope_f = keep.tile([P, H], F32, name="slope_f")
-        cap_f = keep.tile([P, H], F32, name="cap_f")
-        warm = keep.tile([P, 1], F32, name="warm")
-        nc.scalar.dma_start(out=slope_raw[:], in_=slope.partition_broadcast(P))
-        nc.scalar.dma_start(out=cap_raw[:], in_=cap.partition_broadcast(P))
-        nc.scalar.activation(out=warm[:], in_=ident[:, 0:1], func=ACT.Exp)
+
+        column = keep.tile([P, 1], BF16, name="column")
+        column_f32 = keep.tile([P, 1], F32, name="column_f32")
+        factors = keep.tile([P, 2 * H], F32, name="factors")
+        slope_of = lambda h: factors[:, h : h + 1]
+        cap_of = lambda h: factors[:, H + h : H + h + 1]
+        table_probe = keep.tile([P, 1], F32, name="table_probe")
+        ones = keep.tile([P, PACK * P], BF16, name="ones", align_bytes=64)
+        ones_codes = keep.tile([P, P], U32, name="ones_codes", align_bytes=64)
+        ones_scales = keep.tile([P, P], U8, name="ones_scales", align_bytes=64)
+        nc.vector.memset(column[:], 0.0)
+        nc.vector.memset(ones[:], 1.0)
+        nc.vector.quantize_mx(out=ones_codes[:].bitcast(FP8X4), scales=ones_scales[:], in_=ones[:])
+        with nc.allow_non_contiguous_dma(reason="sixteen values, one to a partition"):
+            nc.scalar.dma_start(out=column[0:H, 0:1], in_=slope.rearrange("(h o) -> h o", o=1))
+            nc.scalar.dma_start(out=column[H : 2 * H, 0:1], in_=cap.rearrange("(h o) -> h o", o=1))
+
+        nc.scalar.activation(out=table_probe[:], in_=ones[:, 0:1], func=FUNC.Exp)
+        for i in range(WARM_PASSES):
+            nc.tensor.matmul_mx(
+                out=banks[:, 0, (i % PACK) * P : (i % PACK + 1) * P],
+                lhsT=ones_codes[:].bitcast(FP8X4),
+                lhsT_scale=ones_scales[:],
+                rhs=ones_codes[:].bitcast(FP8X4),
+                rhs_scale=ones_scales[:],
+                start=True,
+                stop=True,
+            )
 
         k_raw = keep.tile([P, GROUPS, PACK, D], BF16, name="k_raw")
         q_raw = keep.tile([P, H, D], BF16, name="q_raw")
@@ -110,110 +190,180 @@ def tile_softcap_multiquery_exp_scores_g2_kernel(tc, queries, keys, slope, cap, 
         q_scales = keep.tile([P, H, PASSES * P], U8, name="q_scales", align_bytes=64)
         y_scales = keep.tile([P, GROUPS, H * L], U8, name="y_scales", align_bytes=64)
 
-        def pick(x, k_tile, q_tile):
-            return k_tile[:, x[1], x[2], :] if x[0] == "k" else q_tile[:, x[1], :]
+        def part(tile, of_keys, of_queries):
+            return of_keys[:, tile[1], tile[2], :] if tile[0] == "k" else of_queries[:, tile[1], :]
 
-        for i, x in enumerate(tiles):
-            if i < 16:
-                src = keys_hbm[x[1], :, x[2], :] if x[0] == "k" else queries_hbm[:, x[1], :]
-                nc.sync.dma_start(out=pick(x, k_raw, q_raw), in_=src)
-            elif i % 4 == 0:
-                if x[0] == "k":
-                    nc.sync.dma_start(out=k_raw[:, x[1], :, :], in_=keys_hbm[x[1]])
-                else:
-                    nc.sync.dma_start(out=q_raw[:, x[1] : x[1] + 4, :], in_=queries_hbm[:, x[1] : x[1] + 4, :])
+        for i, tile in enumerate(tiles):
+            if i < SINGLE_LOADS:
+                nc.sync.dma_start(out=part(tile, k_raw, q_raw), in_=part(tile, keys_hbm.rearrange("g p t d -> p g t d"), queries_hbm))
+            elif tile[0] == "k" and tile[2] == 0:
+                nc.sync.dma_start(out=k_raw[:, tile[1], :, :], in_=keys_hbm[tile[1]])
+            elif tile[0] == "q" and tile[1] % CHUNK_HEADS == 0:
+                heads = slice(tile[1], tile[1] + CHUNK_HEADS)
+                nc.sync.dma_start(out=q_raw[:, heads, :], in_=queries_hbm[:, heads, :])
 
-        nc.vector.tensor_copy(out=slope_f[:], in_=slope_raw[:])
-        nc.vector.tensor_copy(out=cap_f[:], in_=cap_raw[:])
+        grouped, capped, y, y_bf, y_codes = {}, {}, {}, {}, {}
 
-        turned, grouped, scores, capped, y, y_bf, y_codes = {}, {}, {}, {}, {}, {}, {}
+        def y_columns(chunk, lo, hi):
+            owner, place, count = home[chunk]
+            return y[owner][:, place, :, lo:hi]
 
-        def store_scales(m0, m1):
-            for quad in range(4):
-                eng = nc.sync if quad % 2 == 0 or m1 < H * L else nc.scalar
-                eng.dma_start(
-                    out=scales_hbm[:, 4 * quad : 4 * quad + 4, m0 // 4 : m1 // 4].rearrange("g r w -> r g w"),
-                    in_=y_scales[32 * quad : 32 * quad + 4, :, m0:m1].bitcast(I32),
+        def store_scales(g0, g1, m0, m1):
+            for quad in range(QUADRANTS):
+                rows = slice(SCALE_ROWS * quad, SCALE_ROWS * (quad + 1))
+                nc.sync.dma_start(
+                    out=scales_hbm[g0:g1, rows, m0 // 4 : m1 // 4].rearrange("g r w -> r g w"),
+                    in_=y_scales[32 * quad : 32 * quad + SCALE_ROWS, g0:g1, m0:m1].bitcast(I32),
                 )
 
-        for ev in events:
-            kind = ev[0]
-            if kind == "transpose":
-                x = ev[1]
-                words = pick(x, k_raw, q_raw).bitcast(F32)
-                turned[x] = psum.tile([P, PASSES, 2, P], F32, name="turned", tag="turned")
-                for c in range(PASSES):
-                    for u in range(2):
-                        nc.tensor.transpose(turned[x][:, c, u, :], words[:, 256 * c + u : 256 * (c + 1) : 2], ident[:])
-            elif kind == "copy":
-                x = ev[1]
-                grouped[x] = work.tile([P, D], BF16, name="grouped", tag="grouped", bufs=4, align_bytes=64)
-                dst = grouped[x][:].bitcast(F32).rearrange("p (c r u) -> p c r u", c=PASSES, u=2)
-                src = turned[x][:].rearrange("p c u r -> p c r u")
-                if ev[2] == "scalar":
-                    nc.scalar.copy(out=dst, in_=src)
-                else:
-                    nc.vector.tensor_copy(out=dst, in_=src)
-            elif kind == "quant":
-                x = ev[1]
-                nc.vector.quantize_mx(out=pick(x, k_codes, q_codes).bitcast(FP8X4), scales=pick(x, k_scales, q_scales), in_=grouped[x][:])
-            elif kind == "matmul":
-                g, h = units[ev[1]]
-                scores[ev[1]] = psum.tile([P, PACK, L], F32, name="scores", tag="scores")
-                for t in range(PACK):
-                    for c in range(PASSES):
-                        cols = slice(c * P, (c + 1) * P)
-                        nc.tensor.matmul_mx(
-                            out=scores[ev[1]][:, t, :],
-                            lhsT=k_codes[:, g, t, cols].bitcast(FP8X4),
-                            lhsT_scale=k_scales[:, g, t, cols],
-                            rhs=q_codes[:, h, cols].bitcast(FP8X4),
-                            rhs_scale=q_scales[:, h, cols],
-                            start=(c == 0),
-                            stop=(c == PASSES - 1),
-                        )
-            elif kind == "tanh":
-                g, h = units[ev[1]]
-                capped[ev[1]] = work.tile([P, PACK, L], F32, name="capped", tag="capped", bufs=3)
-                nc.scalar.activation(out=capped[ev[1]][:], in_=scores[ev[1]][:], func=ACT.Tanh, scale=slope_f[:, h : h + 1])
-            elif kind == "exp":
-                g, h = units[ev[1]]
-                chunk, j = divmod(ev[1], HEADS_PER_CHUNK)
-                if j == 0:
-                    y[chunk] = work.tile([P, PACK, CHUNK], F32, name="y", tag="y", bufs=6)
-                nc.scalar.activation(out=y[chunk][:, :, j * L : (j + 1) * L], in_=capped[ev[1]][:], func=ACT.Exp, scale=cap_f[:, h : h + 1])
-                m0 = (h - j) * L
-                if chunk == last_chunk:
-                    nc.sync.dma_start(out=y_hbm[g, :, :, h * L : (h + 1) * L], in_=y[chunk][:, :, j * L : (j + 1) * L])
-                elif j == HEADS_PER_CHUNK - 1:
-                    nc.sync.dma_start(out=y_hbm[g, :, :, m0 : m0 + CHUNK], in_=y[chunk][:])
-            elif kind == "cast":
-                chunk, j = divmod(ev[1], HEADS_PER_CHUNK)
-                if j == 0:
-                    y_bf[chunk] = work.tile([P, CHUNK, PACK], BF16, name="y_bf", tag="y_bf", bufs=3, align_bytes=64)
-                nc.vector.tensor_copy(
-                    out=y_bf[chunk][:, j * L : (j + 1) * L, :],
-                    in_=y[chunk][:, :, j * L : (j + 1) * L].rearrange("p t m -> p m t"),
-                )
+        def transpose(tile, bank):
+            pairs = part(tile, k_raw, q_raw).bitcast(F32)
+            for c in range(PASSES):
+                for u in range(2):
+                    col = (2 * c + u) * P
+                    nc.tensor.transpose(banks[:, bank, col : col + P], pairs[:, 2 * P * c + u : 2 * P * (c + 1) : 2], ident[:])
+
+        def interleave(tile, bank, engine):
+            grouped[tile] = work.tile([P, D], BF16, name="grouped", tag="grouped", bufs=4, align_bytes=64)
+            dst = grouped[tile][:].bitcast(F32).rearrange("p (c r u) -> p c r u", c=PASSES, u=2)
+            src = banks[:, bank, :].rearrange("p (c u r) -> p c r u", c=PASSES, u=2)
+            if engine == "scalar":
+                nc.scalar.copy(out=dst, in_=src)
             else:
-                g, h = units[ev[1]]
-                chunk, j = divmod(ev[1], HEADS_PER_CHUNK)
-                m0 = (h - j) * L
-                if chunk == last_chunk:
-                    lo, hi = j * L, (j + 1) * L
-                elif j == HEADS_PER_CHUNK - 1:
-                    lo, hi = 0, CHUNK
-                else:
-                    continue
-                if lo == 0:
-                    y_codes[chunk] = work.tile([P, CHUNK], U32, name="y_codes", tag="y_codes", bufs=3, align_bytes=64)
-                nc.vector.quantize_mx(
-                    out=y_codes[chunk][:, lo:hi].bitcast(FP8X4),
-                    scales=y_scales[:, g, m0 + lo : m0 + hi],
-                    in_=y_bf[chunk][:, lo:hi, :].rearrange("p m t -> p (m t)"),
+                nc.vector.tensor_copy(out=dst, in_=src)
+
+        def quantise(tile):
+            nc.vector.quantize_mx(
+                out=part(tile, k_codes, q_codes).bitcast(FP8X4),
+                scales=part(tile, k_scales, q_scales),
+                in_=grouped[tile][:],
+            )
+
+        def matmul(f, bank):
+            g, hs, ts = fills[f]
+            for i, (h, t) in enumerate([(h, t) for h in hs for t in ts]):
+                for c in range(PASSES):
+                    cols = slice(c * P, (c + 1) * P)
+                    nc.tensor.matmul_mx(
+                        out=banks[:, bank, i * L : (i + 1) * L],
+                        lhsT=k_codes[:, g, t, cols].bitcast(FP8X4),
+                        lhsT_scale=k_scales[:, g, t, cols],
+                        rhs=q_codes[:, h, cols].bitcast(FP8X4),
+                        rhs_scale=q_scales[:, h, cols],
+                        start=(c == 0),
+                        stop=(c == PASSES - 1),
+                    )
+
+        by_query = lambda ap: ap.rearrange("p (t l) -> p t l", l=L)
+        query_half = lambda half: slice(half * L // 2, (half + 1) * L // 2)
+
+        def tanh(f, bank, half):
+            g, hs, ts = fills[f]
+            if f % 2 == 0:
+                capped[f // 2] = work.tile([P, 2, BANK_WIDTH], F32, name="capped", tag="capped", bufs=3)
+            dst, src = capped[f // 2][:, f % 2, :], banks[:, bank, :]
+            if f == last_fill:
+                cols = query_half(half)
+                nc.scalar.activation(out=by_query(dst)[:, :, cols], in_=by_query(src)[:, :, cols], func=FUNC.Tanh, scale=slope_of(hs[0]))
+            else:
+                for i, h in enumerate(hs):
+                    cols = slice(i * len(ts) * L, (i + 1) * len(ts) * L)
+                    nc.scalar.activation(out=dst[:, cols], in_=src[:, cols], func=FUNC.Tanh, scale=slope_of(h))
+
+        def exp(f, twins):
+            g, hs, ts = fills[f]
+            chunk = chunk_of(g, hs[0])
+            owner, place, count = home[chunk]
+            if owner not in y:
+                y[owner] = work.tile([P, count, PACK, CHUNK], F32, name="y", tag="y%d" % count, bufs=5 if count == 1 else 2)
+            first_col = lambda h: h % CHUNK_HEADS * L
+            src = capped[f // 2][:, f % 2, :]
+            if twins:
+                lo = first_col(hs[0])
+                nc.scalar.activation(
+                    out=y[owner][:, :, :, lo : lo + L],
+                    in_=capped[f // 2][:].rearrange("p i (t l) -> p i t l", l=L),
+                    func=FUNC.Exp,
+                    scale=cap_of(hs[0]),
                 )
-                nc.sync.dma_start(out=words_hbm[g, :, m0 + lo : m0 + hi], in_=y_codes[chunk][:, lo:hi].bitcast(I32))
-                if chunk == last_chunk - GROUPS:
-                    store_scales(0, m0 + CHUNK)
-                elif ev[1] == len(units) - 1:
-                    store_scales(m0, m0 + CHUNK)
+            elif f == last_fill:
+                lo = first_col(hs[0])
+                for half in range(2):
+                    cols = query_half(half)
+                    nc.scalar.activation(
+                        out=y_columns(chunk, lo, lo + L)[:, :, cols], in_=by_query(src)[:, :, cols], func=FUNC.Exp, scale=cap_of(hs[0])
+                    )
+            else:
+                for i, h in enumerate(hs):
+                    lo = first_col(h)
+                    nc.scalar.activation(
+                        out=y_columns(chunk, lo, lo + L)[:, ts[0] : ts[-1] + 1, :],
+                        in_=by_query(src[:, i * len(ts) * L : (i + 1) * len(ts) * L]),
+                        func=FUNC.Exp,
+                        scale=cap_of(h),
+                    )
+
+            h = hs[-1]
+            span = 1 if f > last_fill - 2 else 2 if f > last_fill - 2 * CHUNK_HEADS else CHUNK_HEADS
+            if (h + 1) % span == 0 and ts[-1] == PACK - 1:
+                hi = first_col(h) + L
+                for i in range(count):
+                    nc.sync.dma_start(
+                        out=y_hbm[owner[0] + i, :, :, (h + 1 - span) * L : (h + 1) * L],
+                        in_=y[owner][:, i, :, hi - span * L : hi],
+                    )
+
+        def round_to_bf16(g, h):
+            chunk = chunk_of(g, h)
+            lo = h % CHUNK_HEADS * L
+            if chunk not in y_bf:
+                y_bf[chunk] = work.tile([P, CHUNK, PACK], BF16, name="y_bf", tag="y_bf", bufs=4, align_bytes=64)
+            if (g, h) == (GROUPS - 1, H - 1):
+                spans = [(lo, lo + L // 2), (lo + L // 2, lo + L)]
+            elif chunk == last_chunk:
+                spans = [(lo, lo + L)]
+            else:
+                spans = [(lo - L, lo + L)] if h % 2 == 1 else []
+            for a, b in spans:
+                nc.vector.tensor_copy(out=y_bf[chunk][:, a:b, :], in_=y_columns(chunk, a, b).rearrange("p t m -> p m t"))
+
+        def planes(g, h):
+            chunk = chunk_of(g, h)
+            span = 2 if chunk == last_chunk else CHUNK_HEADS
+            if (h + 1) % span != 0:
+                return
+            hi = h % CHUNK_HEADS * L + L
+            lo = hi - span * L
+            m0 = chunk[1] * CHUNK
+            if chunk not in y_codes:
+                y_codes[chunk] = work.tile([P, CHUNK], U32, name="y_codes", tag="y_codes", bufs=3, align_bytes=64)
+            nc.vector.quantize_mx(
+                out=y_codes[chunk][:, lo:hi].bitcast(FP8X4),
+                scales=y_scales[:, g, m0 + lo : m0 + hi],
+                in_=y_bf[chunk][:, lo:hi, :].rearrange("p m t -> p (m t)"),
+            )
+            nc.sync.dma_start(out=words_hbm[g, :, m0 + lo : m0 + hi], in_=y_codes[chunk][:, lo:hi].bitcast(I32))
+
+            last_m0 = (COLUMNS - 1) * CHUNK
+            if chunk == (GROUPS - 1, COLUMNS - 2):
+                store_scales(0, GROUPS, 0, last_m0)
+            elif chunk == (GROUPS - 2, COLUMNS - 1):
+                store_scales(0, GROUPS - 1, last_m0, H * L)
+            elif (g, h) == (GROUPS - 1, H - 1):
+                store_scales(GROUPS - 1, GROUPS, last_m0, H * L)
+
+        actions = {
+            "widen": lambda: nc.vector.tensor_copy(out=column_f32[:], in_=column[:]),
+            "spread": lambda: nc.tensor.transpose(banks[:, 1, 0:P], column_f32[:].to_broadcast([P, P]), ident[:]),
+            "factors": lambda: nc.vector.tensor_copy(out=factors[:], in_=banks[:, 1, 0 : 2 * H]),
+            "transpose": transpose,
+            "interleave": interleave,
+            "quantise": quantise,
+            "matmul": matmul,
+            "tanh": tanh,
+            "exp": exp,
+            "round": lambda unit: round_to_bf16(*unit),
+            "planes": lambda unit: planes(*unit),
+        }
+        for step in program(tiles, fills):
+            actions[step[0]](*step[1:])

from contextlib import ExitStack

import concourse.mybir as mybir
from concourse.masks import make_identity

H, L, D, N = 16, 128, 1024, 2048
FLOPS = 2 * N * H * L * D

F32 = mybir.dt.float32
BF16 = mybir.dt.bfloat16
I32 = mybir.dt.int32
U32 = mybir.dt.uint32
U8 = mybir.dt.uint8
FP8X4 = mybir.dt.float8_e4m3fn_x4
FUNC = mybir.ActivationFunctionType

P = 128
PACK = 4
PASSES = D // (P * PACK)
GROUPS = N // (P * PACK)
CHUNK_HEADS = 4
CHUNK = CHUNK_HEADS * L
COLUMNS = H // CHUNK_HEADS
BANKS, BANK_WIDTH = 8, 512
QUADRANTS, SCALE_ROWS = 4, 4

FIRST_TILES = 6
SINGLE_LOADS = 16
TILES_AFTER_FILL = {0: 4, 3: 3, 8: 3, 12: 4, 21: 2, 23: 2, 30: 2, 32: 2, 41: 2, 44: 2}
SCALAR_TILES = (1, 2, 3, 6, 7, 12)
SCORE_BANKS = 4
LATE = 48
RESULT_LAG = 7
WARM_PASSES = 10
WIDEN_AT, SPREAD_AT = 0, 3


def tile_order():
    key_tiles = lambda g: [("k", g, t) for t in range(PACK)]
    head_tiles = lambda c: [("q", h) for h in range(CHUNK_HEADS * c, CHUNK_HEADS * (c + 1))]
    k0, q0 = key_tiles(0), head_tiles(0)
    tiles = [k0[0], q0[0], k0[1], q0[1], k0[2], k0[3], q0[2], q0[3]] + key_tiles(1)
    return tiles + head_tiles(1) + key_tiles(2) + head_tiles(2) + key_tiles(3) + head_tiles(3)


def fill_order():
    every_t = tuple(range(PACK))
    halves = (every_t[:2], every_t[2:])
    chunk_heads = lambda c: range(CHUNK_HEADS * c, CHUNK_HEADS * (c + 1))
    chunk = lambda g, c: [(g, (h,), every_t) for h in chunk_heads(c)]
    twin_chunks = lambda g, c: [(g + i, (h,), every_t) for h in chunk_heads(c) for i in range(2)]
    fills = [(0, (0, 1), ts) for ts in halves] + chunk(0, 0)[2:]
    fills += [(1, hs, ts) for ts in halves for hs in ((0, 1), (2, 3))]
    fills += twin_chunks(0, 1) + chunk(2, 0) + chunk(2, 1) + twin_chunks(0, 2) + chunk(2, 2)
    fills += chunk(3, 0) + chunk(3, 1) + chunk(3, 2)
    for g in range(GROUPS):
        fills += chunk(g, COLUMNS - 1)
    return fills


def first_twin(fills, f):
    return f % 2 == 0 and fills[f][1:] == fills[f + 1][1:]


def program(tiles, fills):
    steps = []
    emptier = lambda i: "scalar" if i in SCALAR_TILES else "vector"

    for i in range(FIRST_TILES):
        bank = BANKS - 1 - i
        steps.append(("transpose", tiles[i], bank))
        if i == SPREAD_AT:
            steps.append(("spread",))
        steps.append(("interleave", tiles[i], bank, emptier(i)))
        if i == WIDEN_AT:
            steps.append(("widen",))
        steps.append(("quantise", tiles[i]))
        if i == SPREAD_AT:
            steps.append(("factors",))

    n_tiles = FIRST_TILES
    results = []
    n_rounded = n_planes = 0
    bank = -1
    for f in range(len(fills) + 1):
        late = f >= LATE
        fresh = range(n_tiles, n_tiles + TILES_AFTER_FILL.get(f, 0))
        n_tiles += len(fresh)
        turn_bank = lambda i: BANKS - 1 - i % (BANKS - SCORE_BANKS)
        if f < len(fills):
            bank = (bank + 1) % (BANKS if late else SCORE_BANKS)
            steps.append(("matmul", f, bank))
            steps += [("transpose", tiles[i], turn_bank(i)) for i in fresh]
            steps.append(("tanh", f, bank, 0))

        planes_due = n_rounded
        if late:
            steps += [("planes", unit) for after, unit in results[n_planes:planes_due]]
            n_planes = planes_due

        if f >= 1 and not first_twin(fills, f - 1):
            twins = f >= 2 and first_twin(fills, f - 2)
            steps.append(("exp", f - 1, twins))
            for g, hs, ts in fills[f - 2 if twins else f - 1 : f]:
                if PACK - 1 in ts:
                    results += [(f, (g, h)) for h in hs]
        if f == len(fills) - 1:
            steps.append(("tanh", f, bank, 1))

        for k in range(len(fresh) + 1):
            if k < len(fresh):
                steps.append(("interleave", tiles[fresh[k]], turn_bank(fresh[k]), emptier(fresh[k])))
            if k >= 1:
                steps.append(("quantise", tiles[fresh[k - 1]]))

        while n_rounded < len(results) and results[n_rounded][0] <= f - (0 if late else RESULT_LAG):
            steps.append(("round", results[n_rounded][1]))
            n_rounded += 1
        steps += [("planes", unit) for after, unit in results[n_planes:planes_due]]
        n_planes = planes_due
    steps += [("planes", unit) for after, unit in results[n_planes:]]
    return steps


def tile_softcap_multiquery_exp_scores_g2_kernel(tc, queries, keys, slope, cap, out_0, out_1, out_2):
    nc = tc.nc
    tiles, fills = tile_order(), fill_order()
    last_fill = len(fills) - 1
    last_chunk = (GROUPS - 1, COLUMNS - 1)
    chunk_of = lambda g, h: (g, h // CHUNK_HEADS)

    y_hbm = out_0.rearrange("(g p t) h l -> g p t (h l)", p=P, t=PACK)
    words_hbm = out_1.rearrange("g p m t -> g p (m t)").bitcast(I32)
    scales_hbm = out_2.bitcast(I32)
    keys_hbm = keys.rearrange("(g p t) d -> g p t d", p=P, t=PACK)
    queries_hbm = queries.rearrange("h l d -> l h d")

    home = {}
    for f in range(0, len(fills), 2):
        if first_twin(fills, f):
            g, hs, ts = fills[f]
            for place in range(2):
                home[chunk_of(g + place, hs[0])] = (chunk_of(g, hs[0]), place, 2)
    for g, hs, ts in fills:
        home.setdefault(chunk_of(g, hs[0]), (chunk_of(g, hs[0]), 0, 1))

    with ExitStack() as ctx:
        keep = ctx.enter_context(tc.tile_pool(name="keep", bufs=1))
        work = ctx.enter_context(tc.tile_pool(name="work", bufs=3))
        psum = ctx.enter_context(tc.psum_pool(name="psum", bufs=1))
        ctx.enter_context(tc.manual_schedule())

        banks = psum.tile([P, BANKS, BANK_WIDTH], F32, name="banks")
        ident = keep.tile([P, P], F32, name="ident")
        make_identity(nc, ident[:])

        column = keep.tile([P, 1], BF16, name="column")
        column_f32 = keep.tile([P, 1], F32, name="column_f32")
        factors = keep.tile([P, 2 * H], F32, name="factors")
        slope_of = lambda h: factors[:, h : h + 1]
        cap_of = lambda h: factors[:, H + h : H + h + 1]
        table_probe = keep.tile([P, 1], F32, name="table_probe")
        ones = keep.tile([P, PACK * P], BF16, name="ones", align_bytes=64)
        ones_codes = keep.tile([P, P], U32, name="ones_codes", align_bytes=64)
        ones_scales = keep.tile([P, P], U8, name="ones_scales", align_bytes=64)
        nc.vector.memset(column[:], 0.0)
        nc.vector.memset(ones[:], 1.0)
        nc.vector.quantize_mx(out=ones_codes[:].bitcast(FP8X4), scales=ones_scales[:], in_=ones[:])
        with nc.allow_non_contiguous_dma(reason="sixteen values, one to a partition"):
            nc.scalar.dma_start(out=column[0:H, 0:1], in_=slope.rearrange("(h o) -> h o", o=1))
            nc.scalar.dma_start(out=column[H : 2 * H, 0:1], in_=cap.rearrange("(h o) -> h o", o=1))

        nc.scalar.activation(out=table_probe[:], in_=ones[:, 0:1], func=FUNC.Exp)
        for i in range(WARM_PASSES):
            nc.tensor.matmul_mx(
                out=banks[:, 0, (i % PACK) * P : (i % PACK + 1) * P],
                lhsT=ones_codes[:].bitcast(FP8X4),
                lhsT_scale=ones_scales[:],
                rhs=ones_codes[:].bitcast(FP8X4),
                rhs_scale=ones_scales[:],
                start=True,
                stop=True,
            )

        k_raw = keep.tile([P, GROUPS, PACK, D], BF16, name="k_raw")
        q_raw = keep.tile([P, H, D], BF16, name="q_raw")
        k_codes = keep.tile([P, GROUPS, PACK, PASSES * P], U32, name="k_codes", align_bytes=64)
        k_scales = keep.tile([P, GROUPS, PACK, PASSES * P], U8, name="k_scales", align_bytes=64)
        q_codes = keep.tile([P, H, PASSES * P], U32, name="q_codes", align_bytes=64)
        q_scales = keep.tile([P, H, PASSES * P], U8, name="q_scales", align_bytes=64)
        y_scales = keep.tile([P, GROUPS, H * L], U8, name="y_scales", align_bytes=64)

        def part(tile, of_keys, of_queries):
            return of_keys[:, tile[1], tile[2], :] if tile[0] == "k" else of_queries[:, tile[1], :]

        for i, tile in enumerate(tiles):
            if i < SINGLE_LOADS:
                nc.sync.dma_start(out=part(tile, k_raw, q_raw), in_=part(tile, keys_hbm.rearrange("g p t d -> p g t d"), queries_hbm))
            elif tile[0] == "k" and tile[2] == 0:
                nc.sync.dma_start(out=k_raw[:, tile[1], :, :], in_=keys_hbm[tile[1]])
            elif tile[0] == "q" and tile[1] % CHUNK_HEADS == 0:
                heads = slice(tile[1], tile[1] + CHUNK_HEADS)
                nc.sync.dma_start(out=q_raw[:, heads, :], in_=queries_hbm[:, heads, :])

        grouped, capped, y, y_bf, y_codes = {}, {}, {}, {}, {}

        def y_columns(chunk, lo, hi):
            owner, place, count = home[chunk]
            return y[owner][:, place, :, lo:hi]

        def store_scales(g0, g1, m0, m1):
            for quad in range(QUADRANTS):
                rows = slice(SCALE_ROWS * quad, SCALE_ROWS * (quad + 1))
                nc.sync.dma_start(
                    out=scales_hbm[g0:g1, rows, m0 // 4 : m1 // 4].rearrange("g r w -> r g w"),
                    in_=y_scales[32 * quad : 32 * quad + SCALE_ROWS, g0:g1, m0:m1].bitcast(I32),
                )

        def transpose(tile, bank):
            pairs = part(tile, k_raw, q_raw).bitcast(F32)
            for c in range(PASSES):
                for u in range(2):
                    col = (2 * c + u) * P
                    nc.tensor.transpose(banks[:, bank, col : col + P], pairs[:, 2 * P * c + u : 2 * P * (c + 1) : 2], ident[:])

        def interleave(tile, bank, engine):
            grouped[tile] = work.tile([P, D], BF16, name="grouped", tag="grouped", bufs=4, align_bytes=64)
            dst = grouped[tile][:].bitcast(F32).rearrange("p (c r u) -> p c r u", c=PASSES, u=2)
            src = banks[:, bank, :].rearrange("p (c u r) -> p c r u", c=PASSES, u=2)
            if engine == "scalar":
                nc.scalar.copy(out=dst, in_=src)
            else:
                nc.vector.tensor_copy(out=dst, in_=src)

        def quantise(tile):
            nc.vector.quantize_mx(
                out=part(tile, k_codes, q_codes).bitcast(FP8X4),
                scales=part(tile, k_scales, q_scales),
                in_=grouped[tile][:],
            )

        def matmul(f, bank):
            g, hs, ts = fills[f]
            for i, (h, t) in enumerate([(h, t) for h in hs for t in ts]):
                for c in range(PASSES):
                    cols = slice(c * P, (c + 1) * P)
                    nc.tensor.matmul_mx(
                        out=banks[:, bank, i * L : (i + 1) * L],
                        lhsT=k_codes[:, g, t, cols].bitcast(FP8X4),
                        lhsT_scale=k_scales[:, g, t, cols],
                        rhs=q_codes[:, h, cols].bitcast(FP8X4),
                        rhs_scale=q_scales[:, h, cols],
                        start=(c == 0),
                        stop=(c == PASSES - 1),
                    )

        by_query = lambda ap: ap.rearrange("p (t l) -> p t l", l=L)
        query_half = lambda half: slice(half * L // 2, (half + 1) * L // 2)

        def tanh(f, bank, half):
            g, hs, ts = fills[f]
            if f % 2 == 0:
                capped[f // 2] = work.tile([P, 2, BANK_WIDTH], F32, name="capped", tag="capped", bufs=3)
            dst, src = capped[f // 2][:, f % 2, :], banks[:, bank, :]
            if f == last_fill:
                cols = query_half(half)
                nc.scalar.activation(out=by_query(dst)[:, :, cols], in_=by_query(src)[:, :, cols], func=FUNC.Tanh, scale=slope_of(hs[0]))
            else:
                for i, h in enumerate(hs):
                    cols = slice(i * len(ts) * L, (i + 1) * len(ts) * L)
                    nc.scalar.activation(out=dst[:, cols], in_=src[:, cols], func=FUNC.Tanh, scale=slope_of(h))

        def exp(f, twins):
            g, hs, ts = fills[f]
            chunk = chunk_of(g, hs[0])
            owner, place, count = home[chunk]
            if owner not in y:
                y[owner] = work.tile([P, count, PACK, CHUNK], F32, name="y", tag="y%d" % count, bufs=5 if count == 1 else 2)
            first_col = lambda h: h % CHUNK_HEADS * L
            src = capped[f // 2][:, f % 2, :]
            if twins:
                lo = first_col(hs[0])
                nc.scalar.activation(
                    out=y[owner][:, :, :, lo : lo + L],
                    in_=capped[f // 2][:].rearrange("p i (t l) -> p i t l", l=L),
                    func=FUNC.Exp,
                    scale=cap_of(hs[0]),
                )
            elif f == last_fill:
                lo = first_col(hs[0])
                for half in range(2):
                    cols = query_half(half)
                    nc.scalar.activation(
                        out=y_columns(chunk, lo, lo + L)[:, :, cols], in_=by_query(src)[:, :, cols], func=FUNC.Exp, scale=cap_of(hs[0])
                    )
            else:
                for i, h in enumerate(hs):
                    lo = first_col(h)
                    nc.scalar.activation(
                        out=y_columns(chunk, lo, lo + L)[:, ts[0] : ts[-1] + 1, :],
                        in_=by_query(src[:, i * len(ts) * L : (i + 1) * len(ts) * L]),
                        func=FUNC.Exp,
                        scale=cap_of(h),
                    )

            h = hs[-1]
            span = 1 if f > last_fill - 2 else 2 if f > last_fill - 2 * CHUNK_HEADS else CHUNK_HEADS
            if (h + 1) % span == 0 and ts[-1] == PACK - 1:
                hi = first_col(h) + L
                for i in range(count):
                    nc.sync.dma_start(
                        out=y_hbm[owner[0] + i, :, :, (h + 1 - span) * L : (h + 1) * L],
                        in_=y[owner][:, i, :, hi - span * L : hi],
                    )

        def round_to_bf16(g, h):
            chunk = chunk_of(g, h)
            lo = h % CHUNK_HEADS * L
            if chunk not in y_bf:
                y_bf[chunk] = work.tile([P, CHUNK, PACK], BF16, name="y_bf", tag="y_bf", bufs=4, align_bytes=64)
            if (g, h) == (GROUPS - 1, H - 1):
                spans = [(lo, lo + L // 2), (lo + L // 2, lo + L)]
            elif chunk == last_chunk:
                spans = [(lo, lo + L)]
            else:
                spans = [(lo - L, lo + L)] if h % 2 == 1 else []
            for a, b in spans:
                nc.vector.tensor_copy(out=y_bf[chunk][:, a:b, :], in_=y_columns(chunk, a, b).rearrange("p t m -> p m t"))

        def planes(g, h):
            chunk = chunk_of(g, h)
            span = 2 if chunk == last_chunk else CHUNK_HEADS
            if (h + 1) % span != 0:
                return
            hi = h % CHUNK_HEADS * L + L
            lo = hi - span * L
            m0 = chunk[1] * CHUNK
            if chunk not in y_codes:
                y_codes[chunk] = work.tile([P, CHUNK], U32, name="y_codes", tag="y_codes", bufs=3, align_bytes=64)
            nc.vector.quantize_mx(
                out=y_codes[chunk][:, lo:hi].bitcast(FP8X4),
                scales=y_scales[:, g, m0 + lo : m0 + hi],
                in_=y_bf[chunk][:, lo:hi, :].rearrange("p m t -> p (m t)"),
            )
            nc.sync.dma_start(out=words_hbm[g, :, m0 + lo : m0 + hi], in_=y_codes[chunk][:, lo:hi].bitcast(I32))

            last_m0 = (COLUMNS - 1) * CHUNK
            if chunk == (GROUPS - 1, COLUMNS - 2):
                store_scales(0, GROUPS, 0, last_m0)
            elif chunk == (GROUPS - 2, COLUMNS - 1):
                store_scales(0, GROUPS - 1, last_m0, H * L)
            elif (g, h) == (GROUPS - 1, H - 1):
                store_scales(GROUPS - 1, GROUPS, last_m0, H * L)

        actions = {
            "widen": lambda: nc.vector.tensor_copy(out=column_f32[:], in_=column[:]),
            "spread": lambda: nc.tensor.transpose(banks[:, 1, 0:P], column_f32[:].to_broadcast([P, P]), ident[:]),
            "factors": lambda: nc.vector.tensor_copy(out=factors[:], in_=banks[:, 1, 0 : 2 * H]),
            "transpose": transpose,
            "interleave": interleave,
            "quantise": quantise,
            "matmul": matmul,
            "tanh": tanh,
            "exp": exp,
            "round": lambda unit: round_to_bf16(*unit),
            "planes": lambda unit: planes(*unit),
        }
        for step in program(tiles, fills):
            actions[step[0]](*step[1:])
